import numpy as np
import ml_dtypes


def mxq(x, axis, fmt="e4m3"):
    dtype, down = {"e4m3": (ml_dtypes.float8_e4m3fn, 7), "e5m2": (ml_dtypes.float8_e5m2, 14)}[fmt]
    v = np.moveaxis(np.asarray(x, np.float32).astype(ml_dtypes.bfloat16).astype(np.float64), axis, -1)
    blocks = v.reshape(v.shape[:-1] + (-1, 32))
    amax = np.abs(blocks).max(-1, keepdims=True)
    byte = np.maximum(np.where(amax > 0, np.frexp(amax)[1] - 1 + 127, 0) - down, 1)
    scale = np.exp2(byte - 127.0)
    codes = (blocks / scale).astype(np.float32).astype(dtype).astype(np.float64)
    return np.moveaxis((codes * scale).reshape(v.shape), -1, axis)


WIDE = False


def mx_kscale(k):
    if not WIDE:
        return np.ones(k)
    levels = np.array([10, -10, 5, -5, 0])
    if k % 512:
        return np.exp2(np.random.permutation(np.resize(levels, k // 32))).repeat(32)
    a = np.empty((k // 512, 16))
    for p in range(k // 512):
        a[p, :8] = np.random.permutation(np.resize(levels, 8))
        for g in range(8):
            far = levels[np.abs(levels - a[p, g]) >= 10]
            a[p, g + 8] = far[np.random.randint(len(far))]
    return np.exp2(a.ravel()).repeat(32)


def f64(x):
    return np.asarray(x).astype(np.float64)


def striped(idx):
    return np.tile(idx.reshape(-1, 16).T, (8, 1)).astype(np.uint16)


def unstriped(offs):
    return offs[:16].T.reshape(-1).astype(np.int64)


E2M1 = np.array([0.0, 0.5, 1.0, 1.5, 2.0, 3.0, 4.0, 6.0, -0.0, -0.5, -1.0, -1.5, -2.0, -3.0, -4.0, -6.0])


def pack_weight(w, fmt):
    k, n = w.shape
    w = f64(np.asarray(w, np.float32).astype(ml_dtypes.bfloat16)).reshape(k // 32, 32, n)
    amax = np.abs(w).max(1)
    if fmt == "e4m3":
        byte = np.frexp(amax)[1] - 1 + 127 - 7
    else:
        mant, ex = np.frexp(amax / 6.0)
        byte = np.where(mant > 0.5, ex, ex - 1) + 127
    byte = np.clip(np.where(amax > 0, byte, 1), 1, 254)
    scaled = (w * np.exp2(127.0 - byte)[:, None, :]).reshape(k, n).astype(np.float32)
    by_word = np.ascontiguousarray(scaled.reshape(k // 512, 128, 4, n).transpose(0, 1, 3, 2))
    if fmt == "e4m3":
        words = by_word.astype(ml_dtypes.float8_e4m3fn).view(np.uint8)
    else:
        c = by_word.astype(ml_dtypes.float4_e2m1fn).view(np.uint8) & 0xF
        words = (c[..., 0::2] | (c[..., 1::2] << 4)).reshape(k // 512, 128, 2 * n)
    return np.ascontiguousarray(words), np.ascontiguousarray(byte.astype(np.uint8).reshape(k // 512, 16, n))


def unpack_weight(words, scales, fmt):
    g, _, n = scales.shape
    words = np.ascontiguousarray(words).reshape(g, 128, n, -1)
    if fmt == "e4m3":
        vals = words.view(ml_dtypes.float8_e4m3fn).astype(np.float64)
    else:
        nib = np.empty((g, 128, n, 4), np.uint8)
        nib[..., 0::2] = words & 0xF
        nib[..., 1::2] = words >> 4
        vals = E2M1[nib]
    vals = vals * np.repeat(np.exp2(scales.astype(np.float64) - 127.0), 8, axis=1)[..., None]
    return vals.transpose(0, 1, 3, 2).reshape(g * 512, n)


def gelu(v):
    return 0.5 * v * (1.0 + np.tanh(np.sqrt(2.0 / np.pi) * (v + 0.044715 * v**3)))


K, H, N, T, S, P, P2 = 1024, 512, 768, 4096, 2048, 1024, 512


def setup_inputs():
    n = np.random.standard_normal
    s = mx_kscale(K)[:, None]
    u = mx_kscale(H)[:, None]
    tab_words, tab_scales = pack_weight(n((K, T)) * s, "e4m3")
    w2_words, w2_scales = pack_weight(n((H, N)) / np.sqrt(H) / u, "e2m1")
    return {
        "tab_words": tab_words,
        "tab_scales": tab_scales,
        "offs": striped(np.random.permutation(T)[:S]),
        "pos1": striped(np.random.permutation(S)[:P]),
        "pos2": striped(np.random.permutation(S)[:P]),
        "pos3": striped(np.random.permutation(P)[:P2]),
        "pos4": striped(np.random.permutation(S)[:P2]),
        "w1": (1.1 * n((K, H)) / np.sqrt(K) / s).astype(np.float32),
        "scene": (0.9 * n((H, S))).astype(np.float32),
        "gain": (np.exp(0.3 * n(H)) * u[:, 0]).astype(np.float32),
        "link": (1.3 * np.exp(0.3 * n(H)) / u[:, 0]).astype(np.float32),
        "w2_words": w2_words,
        "w2_scales": w2_scales,
        "w3": (n((H, N)) / np.sqrt(H) / u).astype(np.float32),
    }


def reference(tab_words, tab_scales, offs, pos1, pos2, pos3, pos4, w1, scene,
              gain, link, w2_words, w2_scales, w3):
    v = unpack_weight(tab_words, tab_scales, "e4m3")[:, unstriped(offs)]
    w2 = unpack_weight(w2_words, w2_scales, "e2m1")
    lin = mxq(f64(w1), 0, "e4m3").T @ v
    h = f64(gain)[:, None] * np.tanh(lin + f64(scene))
    a1 = f64(link)[:, None] * (h[:, unstriped(pos1)] * h[:, unstriped(pos2)])
    a2 = a1[:, unstriped(pos3)] + h[:, unstriped(pos4)]
    aq = mxq(a2, 0, "e4m3")
    mq = mxq(np.abs(a2), 0, "e4m3")
    return w2.T @ aq + mxq(f64(w3), 0, "e4m3").T @ mq

@@ -1,0 +1,223 @@
+from contextlib import ExitStack
+
+import concourse.mybir as mybir
+
+K, H, N, T, S, P1, P2 = 1024, 512, 768, 4096, 2048, 1024, 512
+FLOPS = 2 * K * H * S + 2 * 2 * H * N * P2
+
+F32 = mybir.dt.float32
+BF16 = mybir.dt.bfloat16
+I32 = mybir.dt.int32
+U32 = mybir.dt.uint32
+U16 = mybir.dt.uint16
+U8 = mybir.dt.uint8
+FP8X4 = mybir.dt.float8_e4m3fn_x4
+FP4X4 = mybir.dt.float4_e2m1fn_x4
+ACT = mybir.ActivationFunctionType
+ALU = mybir.AluOpType
+
+P = 128
+PACK = 4
+BANK = 512
+CHUNKS = ((0, 128), (128, 128), (256, 128), (384, 128))
+
+
+def tile_list_burglary_anchor_scores_kernel(
+    tc, tab_words, tab_scales, offs, pos1, pos2, pos3, pos4, w1, scene,
+    gain, link, w2_words, w2_scales, w3, out,
+):
+    nc = tc.nc
+    with ExitStack() as ctx:
+        keep = ctx.enter_context(tc.tile_pool(name="keep", bufs=1))
+        psum = ctx.enter_context(tc.psum_pool(name="psum", bufs=4))
+
+        def load_list(name, src):
+            tile = keep.tile(list(src.shape), U16, name=name)
+            nc.sync.dma_start(tile[:], src)
+            return tile
+
+        def entries(lst, first, count):
+            return lst[:, first // 16 : (first + count) // 16]
+
+        tab_s = keep.tile([P, T], U8, name="tab_s", align_bytes=64)
+        zero_view = tab_s[:].bitcast(I32)
+        nc.gpsimd.memset(zero_view[:, 0:512], 0)
+        nc.vector.memset(zero_view[:, 512:1024], 0)
+        idx = load_list("idx", offs)
+        p1 = load_list("p1", pos1)
+        p2 = load_list("p2", pos2)
+        for q in range(4):
+            nc.sync.dma_start(
+                out=tab_s[32 * q : 32 * q + 8, :].bitcast(I32),
+                in_=tab_scales[:, 4 * q : 4 * q + 4, :].bitcast(I32),
+            )
+        tab_w = []
+        w1_raw = []
+        for a in range(2):
+            words = keep.tile([P, T], I32, name=f"tab_w{a}", align_bytes=64)
+            nc.sync.dma_start(out=words[:], in_=tab_words[a].rearrange("p t i -> p (t i)").bitcast(I32))
+            tab_w.append(words)
+            raw = keep.tile([P, PACK, H], F32, name=f"w1_raw{a}", align_bytes=64)
+            nc.sync.dma_start(out=raw[:], in_=w1[512 * a : 512 * (a + 1), :].rearrange("(p i) c -> p i c", i=PACK))
+            w1_raw.append(raw)
+
+        scene_rows = scene.rearrange("(p t) j -> p t j", t=PACK)
+        gain_t = keep.tile([P, PACK], F32, name="gain_t")
+        link_t = keep.tile([P, PACK], F32, name="link_t")
+        pre = {}
+
+        def load_scene(t):
+            for c in range(S // BANK):
+                tile = keep.tile([P, BANK], F32, name=f"pre{t}_{c}", align_bytes=64)
+                nc.sync.dma_start(out=tile[:], in_=scene_rows[:, t, c * BANK : (c + 1) * BANK])
+                pre[t, c] = tile
+
+        load_scene(0)
+        nc.sync.dma_start(out=gain_t[:], in_=gain.rearrange("(p t) -> p t", t=PACK))
+        load_scene(1)
+        nc.sync.dma_start(out=link_t[:], in_=link.rearrange("(p t) -> p t", t=PACK))
+        load_scene(2)
+        load_scene(3)
+        p3 = load_list("p3", pos3)
+        p4 = load_list("p4", pos4)
+
+        w3_raw = []
+        for g in range(3):
+            raw = keep.tile([P, PACK, 256], F32, name=f"w3_raw{g}", align_bytes=64)
+            nc.sync.dma_start(out=raw[:], in_=w3[:, 256 * g : 256 * (g + 1)].rearrange("(p i) c -> p i c", i=PACK))
+            w3_raw.append(raw)
+        w2_w = keep.tile([P, 2 * N], U8, name="w2_w", align_bytes=64)
+        nc.sync.dma_start(out=w2_w[:].bitcast(I32), in_=w2_words[0].bitcast(I32))
+        w2_s = keep.tile([P, N], U8, name="w2_s", align_bytes=64)
+        nc.gpsimd.memset(w2_s[:].bitcast(I32), 0)
+        for q in range(4):
+            nc.sync.dma_start(
+                out=w2_s[32 * q : 32 * q + 4, :].bitcast(I32),
+                in_=w2_scales[0, 4 * q : 4 * q + 4, :].bitcast(I32),
+            )
+
+        v_s = keep.tile([P, S], U8, name="v_s", align_bytes=64)
+        nc.vector.tensor_copy(v_s[:], tab_s[:].indirect(idx[:]))
+        v_w0 = keep.tile([P, S], U32, name="v_w0", align_bytes=64)
+        nc.vector.tensor_copy(v_w0[:], tab_w[0][:].bitcast(U32).indirect(idx[:]))
+
+        w1_c = {}
+        w1_s = {}
+
+        def quantise_w1(a, t0, nt):
+            grouped = keep.tile([P, nt, P, PACK], BF16, name=f"w1_g{a}_{t0}", tag=f"stage{3 * a + t0}", align_bytes=64)
+            src = w1_raw[a][:].rearrange("p i (m t) -> p m i t", t=PACK)[:, :, :, t0 : t0 + nt]
+            nc.scalar.copy(out=grouped[:].rearrange("p t m i -> p m i t"), in_=src)
+            codes = keep.tile([P, nt * P], U32, name=f"w1_c{a}_{t0}", align_bytes=64)
+            scales = keep.tile([P, nt * P], U8, name=f"w1_s{a}_{t0}", align_bytes=64)
+            nc.vector.quantize_mx(
+                out=codes[:].bitcast(FP8X4), scales=scales[:], in_=grouped[:].rearrange("p t m i -> p (t m i)")
+            )
+            for t in range(nt):
+                w1_c[a, t0 + t] = codes[:, t * P : (t + 1) * P]
+                w1_s[a, t0 + t] = scales[:, t * P : (t + 1) * P]
+
+        quantise_w1(0, 0, 4)
+        quantise_w1(1, 0, 2)
+        quantise_w1(1, 2, 2)
+
+        h = [keep.tile([P, S], F32, name=f"h{t}", align_bytes=64) for t in range(PACK)]
+        v_w1 = []
+
+        def features(t, c):
+            cols = slice(c * BANK, (c + 1) * BANK)
+            lin = psum.tile([P, BANK], F32, name="lin")
+            for a, words in ((0, v_w0[:, cols]), (1, v_w1[c][:])):
+                nc.tensor.matmul_mx(
+                    out=lin[:], lhsT=w1_c[a, t].bitcast(FP8X4), lhsT_scale=w1_s[a, t],
+                    rhs=words.bitcast(FP8X4), rhs_scale=v_s[4 * a : P, cols],
+                    start=(a == 0), stop=(a == 1),
+                )
+            x = pre[t, c]
+            nc.vector.tensor_tensor(out=x[:], in0=lin[:], in1=x[:], op=ALU.add)
+            nc.scalar.activation(out=x[:], in_=x[:], func=ACT.Tanh)
+            nc.scalar.activation(out=h[t][:, cols], in_=x[:], func=ACT.Copy, scale=gain_t[:, t : t + 1])
+
+        for c in range(S // BANK):
+            words = keep.tile([P, BANK], U32, name=f"v_w1_{c}", tag=f"stage{c}", align_bytes=64)
+            nc.vector.tensor_copy(words[:], tab_w[1][:].bitcast(U32).indirect(entries(idx, c * BANK, BANK)))
+            v_w1.append(words)
+            features(0, c)
+
+        w3_c = keep.tile([P, N], U32, name="w3_c", align_bytes=64)
+        w3_s = keep.tile([P, N], U8, name="w3_s", align_bytes=64)
+
+        def quantise_w3(g):
+            grouped = keep.tile([P, 256, PACK], BF16, name=f"w3_g{g}", align_bytes=64)
+            nc.scalar.copy(
+                out=grouped[:].rearrange("p (c i) t -> p c t i", i=4),
+                in_=w3_raw[g][:].rearrange("p t (c i) -> p c t i", i=4),
+            )
+            nc.vector.quantize_mx(
+                out=w3_c[:, 256 * g : 256 * (g + 1)].bitcast(FP8X4), scales=w3_s[:, 256 * g : 256 * (g + 1)],
+                in_=grouped[:].rearrange("p c t -> p (c t)"),
+            )
+
+        a1 = []
+        for t in range(PACK):
+            if t + 1 < PACK:
+                for c in range(S // BANK):
+                    features(t + 1, c)
+            first = keep.tile([P, P1], F32, name="first", tag="picked", align_bytes=64)
+            nc.vector.tensor_copy(first[:], h[t][:].indirect(p1[:]))
+            prod = keep.tile([P, P1], F32, name="prod", tag="product", align_bytes=64)
+            nc.vector.tensor_tensor(out=prod[:], in0=h[t][:].indirect(p2[:]), in1=first[:], op=ALU.mult)
+            pairs = keep.tile([P, P1], F32, name=f"a1_{t}", align_bytes=64)
+            nc.scalar.activation(out=pairs[:], in_=prod[:], func=ACT.Copy, scale=link_t[:, t : t + 1])
+            a1.append(pairs)
+            if t > 0:
+                quantise_w3(t - 1)
+
+        out_rows = out.rearrange("(n p) j -> p n j", p=P)
+        for j0, w in CHUNKS:
+            tag = "picked" if (j0 // w) % 2 == 0 else "product"
+            anchor = keep.tile([P, PACK, w], F32, name="anchor", tag=tag, align_bytes=64)
+            a2 = keep.tile([P, PACK, w], F32, name=f"a2_{j0}", align_bytes=64)
+            for t in range(PACK):
+                nc.vector.tensor_copy(anchor[:, t, :], h[t][:].indirect(entries(p4, j0, w)))
+            for t in range(PACK):
+                nc.vector.tensor_tensor(
+                    out=a2[:, t, :], in0=a1[t][:].indirect(entries(p3, j0, w)),
+                    in1=anchor[:, t, :], op=ALU.add,
+                )
+            grouped = keep.tile([P, 2, w, PACK], BF16, name="grouped", tag=tag, align_bytes=64)
+            src = a2[:].rearrange("p t (c i) -> p c t i", i=4)
+            signed = grouped[:, 0].rearrange("p (c i) t -> p c t i", i=4)
+            if j0 + w == P2:
+                nc.vector.tensor_copy(out=signed, in_=src)
+            else:
+                nc.scalar.copy(out=signed, in_=src)
+            nc.scalar.activation(out=grouped[:, 1].rearrange("p (c i) t -> p c t i", i=4), in_=src, func=ACT.Abs)
+            codes = keep.tile([P, 2 * w], U32, name=f"a2_c{j0}", align_bytes=64)
+            scales = keep.tile([P, 2 * w], U8, name=f"a2_s{j0}", align_bytes=64)
+            nc.vector.quantize_mx(
+                out=codes[:].bitcast(FP8X4), scales=scales[:], in_=grouped[:].rearrange("p u j t -> p (u j t)")
+            )
+            per_bank = 2 if w == 256 else 3
+            for n0 in range(0, N // P, per_bank):
+                acc = psum.tile([P, BANK], F32, name="acc")
+                for k in range(per_bank):
+                    n = n0 + k
+                    dst = acc[:, k * w : (k + 1) * w]
+                    nc.tensor.matmul_mx(
+                        out=dst, lhsT=w2_w[:, 2 * P * n : 2 * P * (n + 1)].bitcast(FP4X4),
+                        lhsT_scale=w2_s[:, P * n : P * (n + 1)],
+                        rhs=codes[:, 0:w].bitcast(FP8X4), rhs_scale=scales[:, 0:w], start=True, stop=False,
+                    )
+                    nc.tensor.matmul_mx(
+                        out=dst, lhsT=w3_c[:, P * n : P * (n + 1)].bitcast(FP8X4),
+                        lhsT_scale=w3_s[:, P * n : P * (n + 1)],
+                        rhs=codes[:, w : 2 * w].bitcast(FP8X4), rhs_scale=scales[:, w : 2 * w], start=False, stop=True,
+                    )
+                staged = keep.tile([P, per_bank, w], F32, name="staged", bufs=4, align_bytes=64)
+                flat = staged[:].rearrange("p k j -> p (k j)")
+                if j0 + w == P2 and n0 > 0:
+                    nc.vector.tensor_copy(out=flat, in_=acc[:, 0 : per_bank * w])
+                else:
+                    nc.scalar.copy(out=flat, in_=acc[:, 0 : per_bank * w])
+                nc.sync.dma_start(out=out_rows[:, n0 : n0 + per_bank, j0 : j0 + w], in_=staged[:])

@@ -67,10 +67,11 @@ def tile_list_burglary_anchor_scores_kernel(
         pre = {}
 
         def load_scene(t):
-            for c in range(S // BANK):
-                tile = keep.tile([P, BANK], F32, name=f"pre{t}_{c}", align_bytes=64)
-                nc.sync.dma_start(out=tile[:], in_=scene_rows[:, t, c * BANK : (c + 1) * BANK])
-                pre[t, c] = tile
+            width = BANK if t == 0 else 2 * BANK
+            for j in range(0, S, width):
+                tile = keep.tile([P, width], F32, name=f"pre{t}_{j}", tag=f"pre{t}_{j}", align_bytes=64)
+                nc.sync.dma_start(out=tile[:], in_=scene_rows[:, t, j : j + width])
+                pre[t, j] = tile
 
         load_scene(0)
         nc.sync.dma_start(out=gain_t[:], in_=gain.rearrange("(p t) -> p t", t=PACK))
@@ -133,10 +134,14 @@ def tile_list_burglary_anchor_scores_kernel(
                     rhs=words.bitcast(FP8X4), rhs_scale=v_s[4 * a : P, cols],
                     start=(a == 0), stop=(a == 1),
                 )
-            x = pre[t, c]
-            nc.vector.tensor_tensor(out=x[:], in0=lin[:], in1=x[:], op=ALU.add)
-            nc.scalar.activation(out=x[:], in_=x[:], func=ACT.Tanh)
-            nc.scalar.activation(out=h[t][:, cols], in_=x[:], func=ACT.Copy, scale=gain_t[:, t : t + 1])
+            width = BANK if t == 0 else 2 * BANK
+            j = c * BANK // width * width
+            x = pre[t, j]
+            part = x[:, c * BANK - j : (c + 1) * BANK - j]
+            nc.vector.tensor_tensor(out=part, in0=lin[:], in1=part, op=ALU.add)
+            if (c + 1) * BANK == j + width:
+                nc.scalar.activation(out=x[:], in_=x[:], func=ACT.Tanh)
+                nc.scalar.activation(out=h[t][:, j : j + width], in_=x[:], func=ACT.Copy, scale=gain_t[:, t : t + 1])
 
         for c in range(S // BANK):
             words = keep.tile([P, BANK], U32, name=f"v_w1_{c}", tag=f"stage{c}", align_bytes=64)
@@ -163,23 +168,36 @@ def tile_list_burglary_anchor_scores_kernel(
             if t + 1 < PACK:
                 for c in range(S // BANK):
                     features(t + 1, c)
-            first = keep.tile([P, P1], F32, name="first", tag="picked", align_bytes=64)
+            first = keep.tile([P, P1], F32, name="first", bufs=2, align_bytes=64)
             nc.vector.tensor_copy(first[:], h[t][:].indirect(p1[:]))
-            prod = keep.tile([P, P1], F32, name="prod", tag="product", align_bytes=64)
-            nc.vector.tensor_tensor(out=prod[:], in0=h[t][:].indirect(p2[:]), in1=first[:], op=ALU.mult)
             pairs = keep.tile([P, P1], F32, name=f"a1_{t}", align_bytes=64)
-            nc.scalar.activation(out=pairs[:], in_=prod[:], func=ACT.Copy, scale=link_t[:, t : t + 1])
+            for j in range(0, P1, BANK):
+                second = keep.tile([P, BANK], F32, name="second", bufs=4, align_bytes=64)
+                nc.vector.tensor_copy(second[:], h[t][:].indirect(entries(p2, j, BANK)))
+                prod = keep.tile([P, BANK], F32, name="prod", bufs=3, align_bytes=64)
+                nc.gpsimd.tensor_tensor(out=prod[:], in0=first[:, j : j + BANK], in1=second[:], op=ALU.mult)
+                nc.gpsimd.tensor_scalar(
+                    out=pairs[:, j : j + BANK], in0=prod[:], scalar1=link_t[:, t : t + 1], scalar2=0.0,
+                    op0=ALU.mult, op1=ALU.add,
+                )
             a1.append(pairs)
             if t > 0:
                 quantise_w3(t - 1)
 
         out_rows = out.rearrange("(n p) j -> p n j", p=P)
+        early = keep.tile([P, PACK, 256], F32, name="early", tag=f"pre3_{2 * BANK}", align_bytes=64)
+        for t in range(PACK):
+            nc.vector.tensor_copy(early[:, t, :], h[t][:].indirect(entries(p4, 0, 256)))
         for j0, w in CHUNKS:
-            tag = "picked" if (j0 // w) % 2 == 0 else "product"
-            anchor = keep.tile([P, PACK, w], F32, name="anchor", tag=tag, align_bytes=64)
+            tag = f"tail{j0 // w % 2}"
+            if j0 < 256:
+                anchor = early[:, :, j0 : j0 + w]
+            else:
+                late = keep.tile([P, PACK, w], F32, name="late", tag=tag, align_bytes=64)
+                for t in range(PACK):
+                    nc.vector.tensor_copy(late[:, t, :], h[t][:].indirect(entries(p4, j0, w)))
+                anchor = late[:]
             a2 = keep.tile([P, PACK, w], F32, name=f"a2_{j0}", align_bytes=64)
-            for t in range(PACK):
-                nc.vector.tensor_copy(anchor[:, t, :], h[t][:].indirect(entries(p4, j0, w)))
             for t in range(PACK):
                 nc.vector.tensor_tensor(
                     out=a2[:, t, :], in0=a1[t][:].indirect(entries(p3, j0, w)),

@@ -19,7 +19,6 @@ ALU = mybir.AluOpType
 P = 128
 PACK = 4
 BANK = 512
-CHUNKS = ((0, 128), (128, 128), (256, 128), (384, 128))
 
 
 def tile_list_burglary_anchor_scores_kernel(
@@ -57,6 +56,7 @@ def tile_list_burglary_anchor_scores_kernel(
             words = keep.tile([P, T], I32, name=f"tab_w{a}", align_bytes=64)
             nc.sync.dma_start(out=words[:], in_=tab_words[a].rearrange("p t i -> p (t i)").bitcast(I32))
             tab_w.append(words)
+        for a in range(2):
             raw = keep.tile([P, PACK, H], F32, name=f"w1_raw{a}", align_bytes=64)
             nc.sync.dma_start(out=raw[:], in_=w1[512 * a : 512 * (a + 1), :].rearrange("(p i) c -> p i c", i=PACK))
             w1_raw.append(raw)
@@ -106,7 +106,7 @@ def tile_list_burglary_anchor_scores_kernel(
         w1_s = {}
 
         def quantise_w1(a, t0, nt):
-            grouped = keep.tile([P, nt, P, PACK], BF16, name=f"w1_g{a}_{t0}", tag=f"stage{3 * a + t0}", align_bytes=64)
+            grouped = keep.tile([P, nt, P, PACK], BF16, name=f"w1_g{a}_{t0}", tag=f"stage{a}_{t0}", align_bytes=64)
             src = w1_raw[a][:].rearrange("p i (m t) -> p m i t", t=PACK)[:, :, :, t0 : t0 + nt]
             nc.scalar.copy(out=grouped[:].rearrange("p t m i -> p m i t"), in_=src)
             codes = keep.tile([P, nt * P], U32, name=f"w1_c{a}_{t0}", align_bytes=64)
@@ -118,8 +118,9 @@ def tile_list_burglary_anchor_scores_kernel(
                 w1_c[a, t0 + t] = codes[:, t * P : (t + 1) * P]
                 w1_s[a, t0 + t] = scales[:, t * P : (t + 1) * P]
 
-        quantise_w1(0, 0, 4)
+        quantise_w1(0, 0, 2)
         quantise_w1(1, 0, 2)
+        quantise_w1(0, 2, 2)
         quantise_w1(1, 2, 2)
 
         h = [keep.tile([P, S], F32, name=f"h{t}", align_bytes=64) for t in range(PACK)]
@@ -128,7 +129,7 @@ def tile_list_burglary_anchor_scores_kernel(
         def features(t, c):
             cols = slice(c * BANK, (c + 1) * BANK)
             lin = psum.tile([P, BANK], F32, name="lin")
-            for a, words in ((0, v_w0[:, cols]), (1, v_w1[c][:])):
+            for a, words in ((0, v_w0[:, cols]), (1, v_w1[c])):
                 nc.tensor.matmul_mx(
                     out=lin[:], lhsT=w1_c[a, t].bitcast(FP8X4), lhsT_scale=w1_s[a, t],
                     rhs=words.bitcast(FP8X4), rhs_scale=v_s[4 * a : P, cols],
@@ -143,10 +144,12 @@ def tile_list_burglary_anchor_scores_kernel(
                 nc.scalar.activation(out=x[:], in_=x[:], func=ACT.Tanh)
                 nc.scalar.activation(out=h[t][:, j : j + width], in_=x[:], func=ACT.Copy, scale=gain_t[:, t : t + 1])
 
+        for j, count, tag in ((0, 3 * BANK, "v_w1"), (3 * BANK, BANK, "stage0_0")):
+            words = keep.tile([P, count], U32, name="v_w1", tag=tag, align_bytes=64)
+            nc.vector.tensor_copy(words[:], tab_w[1][:].bitcast(U32).indirect(entries(idx, j, count)))
+            for first in range(0, count, BANK):
+                v_w1.append(words[:, first : first + BANK])
         for c in range(S // BANK):
-            words = keep.tile([P, BANK], U32, name=f"v_w1_{c}", tag=f"stage{c}", align_bytes=64)
-            nc.vector.tensor_copy(words[:], tab_w[1][:].bitcast(U32).indirect(entries(idx, c * BANK, BANK)))
-            v_w1.append(words)
             features(0, c)
 
         w3_c = keep.tile([P, N], U32, name="w3_c", align_bytes=64)
@@ -168,74 +171,97 @@ def tile_list_burglary_anchor_scores_kernel(
             if t + 1 < PACK:
                 for c in range(S // BANK):
                     features(t + 1, c)
-            first = keep.tile([P, P1], F32, name="first", bufs=2, align_bytes=64)
+            first = keep.tile([P, P1], F32, name="first", align_bytes=64)
             nc.vector.tensor_copy(first[:], h[t][:].indirect(p1[:]))
-            pairs = keep.tile([P, P1], F32, name=f"a1_{t}", align_bytes=64)
-            for j in range(0, P1, BANK):
-                second = keep.tile([P, BANK], F32, name="second", bufs=4, align_bytes=64)
-                nc.vector.tensor_copy(second[:], h[t][:].indirect(entries(p2, j, BANK)))
-                prod = keep.tile([P, BANK], F32, name="prod", bufs=3, align_bytes=64)
-                nc.gpsimd.tensor_tensor(out=prod[:], in0=first[:, j : j + BANK], in1=second[:], op=ALU.mult)
-                nc.gpsimd.tensor_scalar(
-                    out=pairs[:, j : j + BANK], in0=prod[:], scalar1=link_t[:, t : t + 1], scalar2=0.0,
-                    op0=ALU.mult, op1=ALU.add,
-                )
+            prod = keep.tile([P, P1], F32, name="prod", tag=f"prod{t % 2}", align_bytes=64)
+            nc.vector.tensor_tensor(out=prod[:], in0=h[t][:].indirect(p2[:]), in1=first[:], op=ALU.mult)
+            pairs = keep.tile([P, P1], F32, name=f"a1_{t}", tag=f"pre{t + 1}_{2 * BANK}", align_bytes=64)
+            nc.scalar.activation(out=pairs[:], in_=prod[:], func=ACT.Copy, scale=link_t[:, t : t + 1])
             a1.append(pairs)
-            if t > 0:
-                quantise_w3(t - 1)
+        for g in range(3):
+            quantise_w3(g)
 
         out_rows = out.rearrange("(n p) j -> p n j", p=P)
-        early = keep.tile([P, PACK, 256], F32, name="early", tag=f"pre3_{2 * BANK}", align_bytes=64)
-        for t in range(PACK):
-            nc.vector.tensor_copy(early[:, t, :], h[t][:].indirect(entries(p4, 0, 256)))
-        for j0, w in CHUNKS:
-            tag = f"tail{j0 // w % 2}"
-            if j0 < 256:
-                anchor = early[:, :, j0 : j0 + w]
-            else:
-                late = keep.tile([P, PACK, w], F32, name="late", tag=tag, align_bytes=64)
-                for t in range(PACK):
-                    nc.vector.tensor_copy(late[:, t, :], h[t][:].indirect(entries(p4, j0, w)))
-                anchor = late[:]
-            a2 = keep.tile([P, PACK, w], F32, name=f"a2_{j0}", align_bytes=64)
+
+        def kept_pairs(j0, w, anchor_tag, sum_tag):
+            anchor = keep.tile([P, PACK, w], F32, name="anchor", tag=anchor_tag, align_bytes=64)
+            for t in range(PACK):
+                nc.vector.tensor_copy(anchor[:, t, :], h[t][:].indirect(entries(p4, j0, w)))
+            a2 = keep.tile([P, PACK, w], F32, name="a2", tag=sum_tag, align_bytes=64)
             for t in range(PACK):
                 nc.vector.tensor_tensor(
-                    out=a2[:, t, :], in0=a1[t][:].indirect(entries(p3, j0, w)),
-                    in1=anchor[:, t, :], op=ALU.add,
+                    out=a2[:, t, :], in0=a1[t][:].indirect(entries(p3, j0, w)), in1=anchor[:, t, :], op=ALU.add
                 )
-            grouped = keep.tile([P, 2, w, PACK], BF16, name="grouped", tag=tag, align_bytes=64)
-            src = a2[:].rearrange("p t (c i) -> p c t i", i=4)
-            signed = grouped[:, 0].rearrange("p (c i) t -> p c t i", i=4)
-            if j0 + w == P2:
-                nc.vector.tensor_copy(out=signed, in_=src)
-            else:
-                nc.scalar.copy(out=signed, in_=src)
-            nc.scalar.activation(out=grouped[:, 1].rearrange("p (c i) t -> p c t i", i=4), in_=src, func=ACT.Abs)
-            codes = keep.tile([P, 2 * w], U32, name=f"a2_c{j0}", align_bytes=64)
-            scales = keep.tile([P, 2 * w], U8, name=f"a2_s{j0}", align_bytes=64)
-            nc.vector.quantize_mx(
-                out=codes[:].bitcast(FP8X4), scales=scales[:], in_=grouped[:].rearrange("p u j t -> p (u j t)")
+            return a2[:].rearrange("p t (c i) -> p c t i", i=4)
+
+        def interleaved(tile):
+            return tile.rearrange("p (c i) t -> p c t i", i=4)
+
+        def quantise(name, grouped, width):
+            codes = keep.tile([P, width], U32, name=f"{name}_c", tag=f"{name}_c", align_bytes=64)
+            scales = keep.tile([P, width], U8, name=f"{name}_s", align_bytes=64)
+            nc.vector.quantize_mx(out=codes[:].bitcast(FP8X4), scales=scales[:], in_=grouped)
+            return codes, scales
+
+        def signed_pass(dst, n, codes, scales, start):
+            nc.tensor.matmul_mx(
+                out=dst, lhsT=w2_w[:, 2 * P * n : 2 * P * (n + 1)].bitcast(FP4X4),
+                lhsT_scale=w2_s[:, P * n : P * (n + 1)],
+                rhs=codes.bitcast(FP8X4), rhs_scale=scales, start=start, stop=False,
             )
-            per_bank = 2 if w == 256 else 3
-            for n0 in range(0, N // P, per_bank):
-                acc = psum.tile([P, BANK], F32, name="acc")
-                for k in range(per_bank):
-                    n = n0 + k
-                    dst = acc[:, k * w : (k + 1) * w]
-                    nc.tensor.matmul_mx(
-                        out=dst, lhsT=w2_w[:, 2 * P * n : 2 * P * (n + 1)].bitcast(FP4X4),
-                        lhsT_scale=w2_s[:, P * n : P * (n + 1)],
-                        rhs=codes[:, 0:w].bitcast(FP8X4), rhs_scale=scales[:, 0:w], start=True, stop=False,
-                    )
-                    nc.tensor.matmul_mx(
-                        out=dst, lhsT=w3_c[:, P * n : P * (n + 1)].bitcast(FP8X4),
-                        lhsT_scale=w3_s[:, P * n : P * (n + 1)],
-                        rhs=codes[:, w : 2 * w].bitcast(FP8X4), rhs_scale=scales[:, w : 2 * w], start=False, stop=True,
-                    )
-                staged = keep.tile([P, per_bank, w], F32, name="staged", bufs=4, align_bytes=64)
-                flat = staged[:].rearrange("p k j -> p (k j)")
-                if j0 + w == P2 and n0 > 0:
-                    nc.vector.tensor_copy(out=flat, in_=acc[:, 0 : per_bank * w])
-                else:
-                    nc.scalar.copy(out=flat, in_=acc[:, 0 : per_bank * w])
-                nc.sync.dma_start(out=out_rows[:, n0 : n0 + per_bank, j0 : j0 + w], in_=staged[:])
+
+        def magnitude_pass(dst, n, codes, scales, stop):
+            nc.tensor.matmul_mx(
+                out=dst, lhsT=w3_c[:, P * n : P * (n + 1)].bitcast(FP8X4),
+                lhsT_scale=w3_s[:, P * n : P * (n + 1)],
+                rhs=codes.bitcast(FP8X4), rhs_scale=scales, start=False, stop=stop,
+            )
+
+        def store(acc, n0, count, j0, w, on_vector):
+            staged = keep.tile([P, count, w], F32, name="staged", bufs=5, align_bytes=64)
+            flat = staged[:].rearrange("p k j -> p (k j)")
+            if on_vector:
+                nc.vector.tensor_copy(out=flat, in_=acc[:, 0 : count * w])
+            else:
+                nc.scalar.copy(out=flat, in_=acc[:, 0 : count * w])
+            nc.sync.dma_start(out=out_rows[:, n0 : n0 + count, j0 : j0 + w], in_=staged[:])
+
+        def scores_by_operand(j0, w, src, tags, bank_name, vector_rounds, vector_banks):
+            signed_tag, magnitude_tag, codes_tag = tags
+            signed = keep.tile([P, w, PACK], BF16, name="signed", tag=signed_tag, align_bytes=64)
+            if vector_rounds:
+                nc.vector.tensor_copy(out=interleaved(signed[:]), in_=src)
+            else:
+                nc.scalar.copy(out=interleaved(signed[:]), in_=src)
+            magnitude = keep.tile([P, w, PACK], BF16, name="magnitude", tag=magnitude_tag, align_bytes=64)
+            nc.scalar.activation(out=interleaved(magnitude[:]), in_=src, func=ACT.Abs)
+            s_codes, s_scales = quantise(f"signed{j0}", signed[:].rearrange("p j t -> p (j t)"), w)
+            m_codes, m_scales = quantise(codes_tag, magnitude[:].rearrange("p j t -> p (j t)"), w)
+            banks = [psum.tile([P, BANK], F32, name=bank_name) for b in range(3)]
+            for n in range(N // P):
+                signed_pass(banks[n // 2][:, n % 2 * w : (n % 2 + 1) * w], n, s_codes[:], s_scales[:], n % 2 == 0)
+            for n in range(N // P):
+                magnitude_pass(banks[n // 2][:, n % 2 * w : (n % 2 + 1) * w], n, m_codes[:], m_scales[:], n % 2 == 1)
+                if n % 2 == 1:
+                    store(banks[n // 2], n - 1, 2, j0, w, n // 2 in vector_banks)
+
+        last_scene = "prod0"
+        src = kept_pairs(0, 256, last_scene, "sum0")
+        scores_by_operand(0, 256, src, ("signed0", "magnitude0", "magnitude0"), "acc", False, ())
+
+        j0, w = 256, 128
+        src = kept_pairs(j0, w, last_scene, "signed0")
+        grouped = keep.tile([P, 2, w, PACK], BF16, name="grouped", tag="round1", align_bytes=64)
+        nc.scalar.copy(out=interleaved(grouped[:, 0]), in_=src)
+        nc.scalar.activation(out=interleaved(grouped[:, 1]), in_=src, func=ACT.Abs)
+        codes, scales = quantise("both", grouped[:].rearrange("p u j t -> p (u j t)"), 2 * w)
+        for b, n0 in enumerate((0, 3)):
+            acc = psum.tile([P, BANK], F32, name="acc")
+            for k in range(3):
+                dst = acc[:, k * w : (k + 1) * w]
+                signed_pass(dst, n0 + k, codes[:, 0:w], scales[:, 0:w], True)
+                magnitude_pass(dst, n0 + k, codes[:, w : 2 * w], scales[:, w : 2 * w], True)
+            store(acc, n0, 3, j0, w, b == 1)
+
+        src = kept_pairs(384, 128, "magnitude0", "round1")
+        scores_by_operand(384, 128, src, ("signed2", "magnitude0_c", "magnitude2"), "lin", True, (1,))

from contextlib import ExitStack

import concourse.mybir as mybir

K, H, N, T, S, P1, P2 = 1024, 512, 768, 4096, 2048, 1024, 512
FLOPS = 2 * K * H * S + 2 * 2 * H * N * P2

F32 = mybir.dt.float32
BF16 = mybir.dt.bfloat16
I32 = mybir.dt.int32
U32 = mybir.dt.uint32
U16 = mybir.dt.uint16
U8 = mybir.dt.uint8
FP8X4 = mybir.dt.float8_e4m3fn_x4
FP4X4 = mybir.dt.float4_e2m1fn_x4
ACT = mybir.ActivationFunctionType
ALU = mybir.AluOpType

P = 128
PACK = 4
BANK = 512


def tile_list_burglary_anchor_scores_kernel(
    tc, tab_words, tab_scales, offs, pos1, pos2, pos3, pos4, w1, scene,
    gain, link, w2_words, w2_scales, w3, out,
):
    nc = tc.nc
    with ExitStack() as ctx:
        keep = ctx.enter_context(tc.tile_pool(name="keep", bufs=1))
        psum = ctx.enter_context(tc.psum_pool(name="psum", bufs=4))

        def load_list(name, src):
            tile = keep.tile(list(src.shape), U16, name=name)
            nc.sync.dma_start(tile[:], src)
            return tile

        def entries(lst, first, count):
            return lst[:, first // 16 : (first + count) // 16]

        tab_s = keep.tile([P, T], U8, name="tab_s", align_bytes=64)
        zero_view = tab_s[:].bitcast(I32)
        nc.gpsimd.memset(zero_view[:, 0:512], 0)
        nc.vector.memset(zero_view[:, 512:1024], 0)
        idx = load_list("idx", offs)
        p1 = load_list("p1", pos1)
        p2 = load_list("p2", pos2)
        for q in range(4):
            nc.sync.dma_start(
                out=tab_s[32 * q : 32 * q + 8, :].bitcast(I32),
                in_=tab_scales[:, 4 * q : 4 * q + 4, :].bitcast(I32),
            )
        tab_w = []
        w1_raw = []
        for a in range(2):
            words = keep.tile([P, T], I32, name=f"tab_w{a}", align_bytes=64)
            nc.sync.dma_start(out=words[:], in_=tab_words[a].rearrange("p t i -> p (t i)").bitcast(I32))
            tab_w.append(words)
        for a in range(2):
            raw = keep.tile([P, PACK, H], F32, name=f"w1_raw{a}", align_bytes=64)
            nc.sync.dma_start(out=raw[:], in_=w1[512 * a : 512 * (a + 1), :].rearrange("(p i) c -> p i c", i=PACK))
            w1_raw.append(raw)

        scene_rows = scene.rearrange("(p t) j -> p t j", t=PACK)
        gain_t = keep.tile([P, PACK], F32, name="gain_t")
        link_t = keep.tile([P, PACK], F32, name="link_t")
        pre = {}

        def load_scene(t):
            width = BANK if t == 0 else 2 * BANK
            for j in range(0, S, width):
                tile = keep.tile([P, width], F32, name=f"pre{t}_{j}", tag=f"pre{t}_{j}", align_bytes=64)
                nc.sync.dma_start(out=tile[:], in_=scene_rows[:, t, j : j + width])
                pre[t, j] = tile

        load_scene(0)
        nc.sync.dma_start(out=gain_t[:], in_=gain.rearrange("(p t) -> p t", t=PACK))
        load_scene(1)
        nc.sync.dma_start(out=link_t[:], in_=link.rearrange("(p t) -> p t", t=PACK))
        load_scene(2)
        load_scene(3)
        p3 = load_list("p3", pos3)
        p4 = load_list("p4", pos4)

        w3_raw = []
        for g in range(3):
            raw = keep.tile([P, PACK, 256], F32, name=f"w3_raw{g}", align_bytes=64)
            nc.sync.dma_start(out=raw[:], in_=w3[:, 256 * g : 256 * (g + 1)].rearrange("(p i) c -> p i c", i=PACK))
            w3_raw.append(raw)
        w2_w = keep.tile([P, 2 * N], U8, name="w2_w", align_bytes=64)
        nc.sync.dma_start(out=w2_w[:].bitcast(I32), in_=w2_words[0].bitcast(I32))
        w2_s = keep.tile([P, N], U8, name="w2_s", align_bytes=64)
        nc.gpsimd.memset(w2_s[:].bitcast(I32), 0)
        for q in range(4):
            nc.sync.dma_start(
                out=w2_s[32 * q : 32 * q + 4, :].bitcast(I32),
                in_=w2_scales[0, 4 * q : 4 * q + 4, :].bitcast(I32),
            )

        v_s = keep.tile([P, S], U8, name="v_s", align_bytes=64)
        nc.vector.tensor_copy(v_s[:], tab_s[:].indirect(idx[:]))
        v_w0 = keep.tile([P, S], U32, name="v_w0", align_bytes=64)
        nc.vector.tensor_copy(v_w0[:], tab_w[0][:].bitcast(U32).indirect(idx[:]))

        w1_c = {}
        w1_s = {}

        def quantise_w1(a, t0, nt):
            grouped = keep.tile([P, nt, P, PACK], BF16, name=f"w1_g{a}_{t0}", tag=f"stage{a}_{t0}", align_bytes=64)
            src = w1_raw[a][:].rearrange("p i (m t) -> p m i t", t=PACK)[:, :, :, t0 : t0 + nt]
            nc.scalar.copy(out=grouped[:].rearrange("p t m i -> p m i t"), in_=src)
            codes = keep.tile([P, nt * P], U32, name=f"w1_c{a}_{t0}", align_bytes=64)
            scales = keep.tile([P, nt * P], U8, name=f"w1_s{a}_{t0}", align_bytes=64)
            nc.vector.quantize_mx(
                out=codes[:].bitcast(FP8X4), scales=scales[:], in_=grouped[:].rearrange("p t m i -> p (t m i)")
            )
            for t in range(nt):
                w1_c[a, t0 + t] = codes[:, t * P : (t + 1) * P]
                w1_s[a, t0 + t] = scales[:, t * P : (t + 1) * P]

        quantise_w1(0, 0, 2)
        quantise_w1(1, 0, 2)
        quantise_w1(0, 2, 2)
        quantise_w1(1, 2, 2)

        h = [keep.tile([P, S], F32, name=f"h{t}", align_bytes=64) for t in range(PACK)]
        v_w1 = []

        def features(t, c):
            cols = slice(c * BANK, (c + 1) * BANK)
            lin = psum.tile([P, BANK], F32, name="lin")
            for a, words in ((0, v_w0[:, cols]), (1, v_w1[c])):
                nc.tensor.matmul_mx(
                    out=lin[:], lhsT=w1_c[a, t].bitcast(FP8X4), lhsT_scale=w1_s[a, t],
                    rhs=words.bitcast(FP8X4), rhs_scale=v_s[4 * a : P, cols],
                    start=(a == 0), stop=(a == 1),
                )
            width = BANK if t == 0 else 2 * BANK
            j = c * BANK // width * width
            x = pre[t, j]
            part = x[:, c * BANK - j : (c + 1) * BANK - j]
            nc.vector.tensor_tensor(out=part, in0=lin[:], in1=part, op=ALU.add)
            if (c + 1) * BANK == j + width:
                nc.scalar.activation(out=x[:], in_=x[:], func=ACT.Tanh)
                nc.scalar.activation(out=h[t][:, j : j + width], in_=x[:], func=ACT.Copy, scale=gain_t[:, t : t + 1])

        for j, count, tag in ((0, 3 * BANK, "v_w1"), (3 * BANK, BANK, "stage0_0")):
            words = keep.tile([P, count], U32, name="v_w1", tag=tag, align_bytes=64)
            nc.vector.tensor_copy(words[:], tab_w[1][:].bitcast(U32).indirect(entries(idx, j, count)))
            for first in range(0, count, BANK):
                v_w1.append(words[:, first : first + BANK])
        for c in range(S // BANK):
            features(0, c)

        w3_c = keep.tile([P, N], U32, name="w3_c", align_bytes=64)
        w3_s = keep.tile([P, N], U8, name="w3_s", align_bytes=64)

        def quantise_w3(g):
            grouped = keep.tile([P, 256, PACK], BF16, name=f"w3_g{g}", align_bytes=64)
            nc.scalar.copy(
                out=grouped[:].rearrange("p (c i) t -> p c t i", i=4),
                in_=w3_raw[g][:].rearrange("p t (c i) -> p c t i", i=4),
            )
            nc.vector.quantize_mx(
                out=w3_c[:, 256 * g : 256 * (g + 1)].bitcast(FP8X4), scales=w3_s[:, 256 * g : 256 * (g + 1)],
                in_=grouped[:].rearrange("p c t -> p (c t)"),
            )

        a1 = []
        for t in range(PACK):
            if t + 1 < PACK:
                for c in range(S // BANK):
                    features(t + 1, c)
            first = keep.tile([P, P1], F32, name="first", align_bytes=64)
            nc.vector.tensor_copy(first[:], h[t][:].indirect(p1[:]))
            prod = keep.tile([P, P1], F32, name="prod", tag=f"prod{t % 2}", align_bytes=64)
            nc.vector.tensor_tensor(out=prod[:], in0=h[t][:].indirect(p2[:]), in1=first[:], op=ALU.mult)
            pairs = keep.tile([P, P1], F32, name=f"a1_{t}", tag=f"pre{t + 1}_{2 * BANK}", align_bytes=64)
            nc.scalar.activation(out=pairs[:], in_=prod[:], func=ACT.Copy, scale=link_t[:, t : t + 1])
            a1.append(pairs)
        for g in range(3):
            quantise_w3(g)

        out_rows = out.rearrange("(n p) j -> p n j", p=P)

        def kept_pairs(j0, w, anchor_tag, sum_tag):
            anchor = keep.tile([P, PACK, w], F32, name="anchor", tag=anchor_tag, align_bytes=64)
            for t in range(PACK):
                nc.vector.tensor_copy(anchor[:, t, :], h[t][:].indirect(entries(p4, j0, w)))
            a2 = keep.tile([P, PACK, w], F32, name="a2", tag=sum_tag, align_bytes=64)
            for t in range(PACK):
                nc.vector.tensor_tensor(
                    out=a2[:, t, :], in0=a1[t][:].indirect(entries(p3, j0, w)), in1=anchor[:, t, :], op=ALU.add
                )
            return a2[:].rearrange("p t (c i) -> p c t i", i=4)

        def interleaved(tile):
            return tile.rearrange("p (c i) t -> p c t i", i=4)

        def quantise(name, grouped, width):
            codes = keep.tile([P, width], U32, name=f"{name}_c", tag=f"{name}_c", align_bytes=64)
            scales = keep.tile([P, width], U8, name=f"{name}_s", align_bytes=64)
            nc.vector.quantize_mx(out=codes[:].bitcast(FP8X4), scales=scales[:], in_=grouped)
            return codes, scales

        def signed_pass(dst, n, codes, scales, start):
            nc.tensor.matmul_mx(
                out=dst, lhsT=w2_w[:, 2 * P * n : 2 * P * (n + 1)].bitcast(FP4X4),
                lhsT_scale=w2_s[:, P * n : P * (n + 1)],
                rhs=codes.bitcast(FP8X4), rhs_scale=scales, start=start, stop=False,
            )

        def magnitude_pass(dst, n, codes, scales, stop):
            nc.tensor.matmul_mx(
                out=dst, lhsT=w3_c[:, P * n : P * (n + 1)].bitcast(FP8X4),
                lhsT_scale=w3_s[:, P * n : P * (n + 1)],
                rhs=codes.bitcast(FP8X4), rhs_scale=scales, start=False, stop=stop,
            )

        def store(acc, n0, count, j0, w, on_vector):
            staged = keep.tile([P, count, w], F32, name="staged", bufs=5, align_bytes=64)
            flat = staged[:].rearrange("p k j -> p (k j)")
            if on_vector:
                nc.vector.tensor_copy(out=flat, in_=acc[:, 0 : count * w])
            else:
                nc.scalar.copy(out=flat, in_=acc[:, 0 : count * w])
            nc.sync.dma_start(out=out_rows[:, n0 : n0 + count, j0 : j0 + w], in_=staged[:])

        def scores_by_operand(j0, w, src, tags, bank_name, vector_rounds, vector_banks):
            signed_tag, magnitude_tag, codes_tag = tags
            signed = keep.tile([P, w, PACK], BF16, name="signed", tag=signed_tag, align_bytes=64)
            if vector_rounds:
                nc.vector.tensor_copy(out=interleaved(signed[:]), in_=src)
            else:
                nc.scalar.copy(out=interleaved(signed[:]), in_=src)
            magnitude = keep.tile([P, w, PACK], BF16, name="magnitude", tag=magnitude_tag, align_bytes=64)
            nc.scalar.activation(out=interleaved(magnitude[:]), in_=src, func=ACT.Abs)
            s_codes, s_scales = quantise(f"signed{j0}", signed[:].rearrange("p j t -> p (j t)"), w)
            m_codes, m_scales = quantise(codes_tag, magnitude[:].rearrange("p j t -> p (j t)"), w)
            banks = [psum.tile([P, BANK], F32, name=bank_name) for b in range(3)]
            for n in range(N // P):
                signed_pass(banks[n // 2][:, n % 2 * w : (n % 2 + 1) * w], n, s_codes[:], s_scales[:], n % 2 == 0)
            for n in range(N // P):
                magnitude_pass(banks[n // 2][:, n % 2 * w : (n % 2 + 1) * w], n, m_codes[:], m_scales[:], n % 2 == 1)
                if n % 2 == 1:
                    store(banks[n // 2], n - 1, 2, j0, w, n // 2 in vector_banks)

        last_scene = "prod0"
        src = kept_pairs(0, 256, last_scene, "sum0")
        scores_by_operand(0, 256, src, ("signed0", "magnitude0", "magnitude0"), "acc", False, ())

        j0, w = 256, 128
        src = kept_pairs(j0, w, last_scene, "signed0")
        grouped = keep.tile([P, 2, w, PACK], BF16, name="grouped", tag="round1", align_bytes=64)
        nc.scalar.copy(out=interleaved(grouped[:, 0]), in_=src)
        nc.scalar.activation(out=interleaved(grouped[:, 1]), in_=src, func=ACT.Abs)
        codes, scales = quantise("both", grouped[:].rearrange("p u j t -> p (u j t)"), 2 * w)
        for b, n0 in enumerate((0, 3)):
            acc = psum.tile([P, BANK], F32, name="acc")
            for k in range(3):
                dst = acc[:, k * w : (k + 1) * w]
                signed_pass(dst, n0 + k, codes[:, 0:w], scales[:, 0:w], True)
                magnitude_pass(dst, n0 + k, codes[:, w : 2 * w], scales[:, w : 2 * w], True)
            store(acc, n0, 3, j0, w, b == 1)

        src = kept_pairs(384, 128, "magnitude0", "round1")
        scores_by_operand(384, 128, src, ("signed2", "magnitude0_c", "magnitude2"), "lin", True, (1,))
